import numpy as np
import ml_dtypes


def mxq(x, axis, fmt="e4m3"):
    dtype, down = {"e4m3": (ml_dtypes.float8_e4m3fn, 7), "e5m2": (ml_dtypes.float8_e5m2, 14)}[fmt]
    v = np.moveaxis(np.asarray(x, np.float32).astype(ml_dtypes.bfloat16).astype(np.float64), axis, -1)
    blocks = v.reshape(v.shape[:-1] + (-1, 32))
    amax = np.abs(blocks).max(-1, keepdims=True)
    byte = np.maximum(np.where(amax > 0, np.frexp(amax)[1] - 1 + 127, 0) - down, 1)
    scale = np.exp2(byte - 127.0)
    codes = (blocks / scale).astype(np.float32).astype(dtype).astype(np.float64)
    return np.moveaxis((codes * scale).reshape(v.shape), -1, axis)


WIDE = False


def mx_kscale(k):
    if not WIDE:
        return np.ones(k)
    levels = np.array([10, -10, 5, -5, 0])
    if k % 512:
        return np.exp2(np.random.permutation(np.resize(levels, k // 32))).repeat(32)
    a = np.empty((k // 512, 16))
    for p in range(k // 512):
        a[p, :8] = np.random.permutation(np.resize(levels, 8))
        for g in range(8):
            far = levels[np.abs(levels - a[p, g]) >= 10]
            a[p, g + 8] = far[np.random.randint(len(far))]
    return np.exp2(a.ravel()).repeat(32)


def f64(x):
    return np.asarray(x).astype(np.float64)


def striped8(idx):
    return np.asarray(idx).reshape(8, -1, 16).transpose(0, 2, 1).reshape(128, -1).astype(np.uint16)


def unstriped8(offs):
    return offs.reshape(8, 16, -1).transpose(0, 2, 1).reshape(8, -1).astype(np.int64)


def pick8(x, idx, run):
    r = np.arange(len(x))
    return x[r[:, None], idx[r % (8 * run) // run]]


E2M1 = np.array([0.0, 0.5, 1.0, 1.5, 2.0, 3.0, 4.0, 6.0, -0.0, -0.5, -1.0, -1.5, -2.0, -3.0, -4.0, -6.0])


def pack_weight(w, fmt):
    k, n = w.shape
    w = f64(np.asarray(w, np.float32).astype(ml_dtypes.bfloat16)).reshape(k // 32, 32, n)
    amax = np.abs(w).max(1)
    if fmt == "e4m3":
        byte = np.frexp(amax)[1] - 1 + 127 - 7
    else:
        mant, ex = np.frexp(amax / 6.0)
        byte = np.where(mant > 0.5, ex, ex - 1) + 127
    byte = np.clip(np.where(amax > 0, byte, 1), 1, 254)
    scaled = (w * np.exp2(127.0 - byte)[:, None, :]).reshape(k, n).astype(np.float32)
    by_word = np.ascontiguousarray(scaled.reshape(k // 512, 128, 4, n).transpose(0, 1, 3, 2))
    if fmt == "e4m3":
        words = by_word.astype(ml_dtypes.float8_e4m3fn).view(np.uint8)
    else:
        c = by_word.astype(ml_dtypes.float4_e2m1fn).view(np.uint8) & 0xF
        words = (c[..., 0::2] | (c[..., 1::2] << 4)).reshape(k // 512, 128, 2 * n)
    return np.ascontiguousarray(words), np.ascontiguousarray(byte.astype(np.uint8).reshape(k // 512, 16, n))


def unpack_weight(words, scales, fmt):
    g, _, n = scales.shape
    words = np.ascontiguousarray(words).reshape(g, 128, n, -1)
    if fmt == "e4m3":
        vals = words.view(ml_dtypes.float8_e4m3fn).astype(np.float64)
    else:
        nib = np.empty((g, 128, n, 4), np.uint8)
        nib[..., 0::2] = words & 0xF
        nib[..., 1::2] = words >> 4
        vals = E2M1[nib]
    vals = vals * np.repeat(np.exp2(scales.astype(np.float64) - 127.0), 8, axis=1)[..., None]
    return vals.transpose(0, 1, 3, 2).reshape(g * 512, n)


def sigmoid(v):
    return 1.0 / (1.0 + np.exp(-v))


D, T, U, X, I, Q, E = 512, 1024, 1024, 1024, 512, 512, 256


def setup_inputs():
    n = np.random.standard_normal
    idx = np.stack([np.random.permutation(T)[:I] for _ in range(8)])
    idx2 = np.stack([np.random.permutation(X)[:I] for _ in range(8)])
    idx3 = np.stack([np.random.permutation(U)[:I] for _ in range(8)])
    idx4 = np.stack([np.random.permutation(U)[:I] for _ in range(8)])
    idx5 = np.stack([np.random.permutation(T)[:I] for _ in range(8)])
    fd = mx_kscale(D)
    fq = mx_kscale(Q)
    keysp = pack_weight(n((D, T)) / fd[:, None], "e4m3")
    notesp = pack_weight(n((D, U)) / fd[:, None], "e2m1")
    usersp = pack_weight(n((D, X)) / fd[:, None], "e2m1")
    mixp = pack_weight(n((Q, E)) * 1.0 / np.sqrt(Q) / fq[:, None], "e2m1")
    return {
        "query": (n((D, Q)) * 1.0 / np.sqrt(D) * fd[:, None]).astype(np.float32),
        "query2": (n((D, Q)) * 1.0 / np.sqrt(D) * fd[:, None]).astype(np.float32),
        "keys_words": keysp[0],
        "keys_scales": keysp[1],
        "notes_words": notesp[0],
        "notes_scales": notesp[1],
        "users_words": usersp[0],
        "users_scales": usersp[1],
        "thr": (np.random.uniform(-0.6, 0.6, (Q, 1))).astype(np.float32),
        "slope": (np.random.uniform(1.0, 3.0, (Q, 1))).astype(np.float32),
        "rowf": (np.random.uniform(0.5, 2.0, (Q, 1)) * fq[:, None]).astype(np.float32),
        "mix_words": mixp[0],
        "mix_scales": mixp[1],
        "offs": striped8(idx),
        "offs2": striped8(idx2),
        "offs3": striped8(idx3),
        "offs4": striped8(idx4),
        "offs5": striped8(idx5),
    }


def reference(query, query2, keys_words, keys_scales, notes_words, notes_scales, users_words, users_scales, thr, slope, rowf, mix_words, mix_scales, offs, offs2, offs3, offs4, offs5):
    idx = unstriped8(offs)
    idx2 = unstriped8(offs2)
    idx3 = unstriped8(offs3)
    idx4 = unstriped8(offs4)
    idx5 = unstriped8(offs5)
    keysu = unpack_weight(keys_words, keys_scales, "e4m3")
    notesu = unpack_weight(notes_words, notes_scales, "e2m1")
    usersu = unpack_weight(users_words, users_scales, "e2m1")
    mixu = unpack_weight(mix_words, mix_scales, "e2m1")
    queryq = mxq(f64(query), 0, "e4m3")
    a = queryq.T @ keysu
    b = queryq.T @ notesu
    query2q = mxq(f64(query2), 0, "e4m3")
    c0 = query2q.T @ usersu
    s1 = sigmoid(pick8(a, idx, 64) * f64(slope) + f64(thr))
    w = pick8(c0, idx2, 64) * s1
    f1 = np.zeros((Q, U))
    f1[np.arange(Q)[:, None], idx3[np.arange(Q) % 512 // 64]] = w
    cc = b + f1
    g = np.maximum(pick8(cc, idx4, 64), pick8(a, idx5, 64))
    gw = g * f64(rowf)
    gwq = mxq(gw, 0, "e4m3")
    y = mixu.T @ gwq
    return y

@@ -1,0 +1,237 @@
+from contextlib import ExitStack
+
+import concourse.mybir as mybir
+
+D, T, Q, I, E = 512, 1024, 512, 512, 256
+P = 128
+PACK = 4
+BANK = 512
+FLOPS = 2 * D * Q * T * 3 + 2 * Q * E * I
+
+F32 = mybir.dt.float32
+BF16 = mybir.dt.bfloat16
+I32 = mybir.dt.int32
+U32 = mybir.dt.uint32
+U16 = mybir.dt.uint16
+U8 = mybir.dt.uint8
+FP8X4 = mybir.dt.float8_e4m3fn_x4
+FP4X4 = mybir.dt.float4_e2m1fn_x4
+MULT = mybir.AluOpType.mult
+ADD = mybir.AluOpType.add
+MAX = mybir.AluOpType.max
+COPY = mybir.ActivationFunctionType.Copy
+SIGMOID = mybir.ActivationFunctionType.Sigmoid
+
+
+def tile_attend_upheld_threeq_mixed_kernel(
+    tc, query, query2, keys_words, keys_scales, notes_words, notes_scales, users_words, users_scales,
+    thr, slope, rowf, mix_words, mix_scales, offs, offs2, offs3, offs4, offs5, out,
+):
+    nc = tc.nc
+    with ExitStack() as ctx:
+        keep = ctx.enter_context(tc.tile_pool(name="keep", bufs=1))
+        psum = ctx.enter_context(tc.psum_pool(name="psum", bufs=1))
+
+        def sb(name, shape, dtype):
+            return keep.tile(shape, dtype, name=name, align_bytes=64)
+
+        def scale_plane(name, width):
+            plane = sb(name, [P, width], U8)
+            return plane
+
+        def load_scales(queue, plane, scales):
+            for quad in range(4):
+                queue.dma_start(plane[32 * quad : 32 * quad + 4, :].bitcast(I32), scales[0, 4 * quad : 4 * quad + 4, :].bitcast(I32))
+
+        def load_list(name, src):
+            lst = sb(name, [P, I // 16], U16)
+            nc.sync.dma_start(lst[:], src)
+            return lst
+
+        def load_rows(queue, name, src):
+            col = sb(name, [P, PACK], F32)
+            queue.dma_start(col[:], src.rearrange("(p t) o -> p (t o)", t=PACK))
+            return col
+
+        def load_query(name, src):
+            halves = []
+            for h in range(2):
+                raw = sb("%s_raw%d" % (name, h), [P, PACK, Q // 2], F32)
+                nc.sync.dma_start(raw[:], src.rearrange("(p j) q -> p j q", j=PACK)[:, :, h * (Q // 2) : (h + 1) * (Q // 2)])
+                halves.append(raw)
+            return halves
+
+        def load_fp4(name, src, width):
+            words = sb(name, [P, 2 * width], U8)
+            nc.sync.dma_start(words[:].bitcast(I32), src[0].bitcast(I32))
+            return words
+
+        keys_sc = scale_plane("keys_sc", T)
+        users_sc = scale_plane("users_sc", T)
+        notes_sc = scale_plane("notes_sc", T)
+        mix_sc = scale_plane("mix_sc", E)
+        f1 = [sb("f1_%d" % k, [P, T], F32) for k in range(2)]
+        slope_t = load_rows(nc.gpsimd, "slope_t", slope)
+        thr_t = load_rows(nc.gpsimd, "thr_t", thr)
+        rowf_t = load_rows(nc.gpsimd, "rowf_t", rowf)
+        for win in f1:
+            nc.gpsimd.memset(win[:], 0.0)
+
+        load_scales(nc.scalar, keys_sc, keys_scales)
+        l1 = load_list("l1", offs)
+        q_raw = load_query("q", query)
+        keys = sb("keys", [P, T], U32)
+        nc.sync.dma_start(keys[:].bitcast(I32), keys_words[0].rearrange("p n r -> p (n r)").bitcast(I32))
+        q2_raw = load_query("q2", query2)
+        users = load_fp4("users", users_words, T)
+        load_scales(nc.sync, users_sc, users_scales)
+        l2 = load_list("l2", offs2)
+        l3 = load_list("l3", offs3)
+        notes = load_fp4("notes", notes_words, T)
+        load_scales(nc.sync, notes_sc, notes_scales)
+        l5 = load_list("l5", offs5)
+        l4 = load_list("l4", offs4)
+        mix = load_fp4("mix", mix_words, E)
+        load_scales(nc.sync, mix_sc, mix_scales)
+
+        def deal(grouped, raw, h):
+            m = P // 2
+            nc.vector.tensor_copy(
+                grouped[:, :, h * m : (h + 1) * m, :].rearrange("p t m j -> p m t j"),
+                raw[h][:].rearrange("p j (m t) -> p m t j", t=PACK),
+            )
+
+        def quantize(codes, scales, grouped, t0, t1):
+            nc.vector.quantize_mx(
+                out=codes[:, t0 * P : t1 * P].bitcast(FP8X4),
+                scales=scales[:, t0 * P : t1 * P],
+                in_=grouped[:, t0:t1, :, :].rearrange("p t m j -> p (t m j)"),
+            )
+
+        banks = [psum.tile([P, BANK], F32, name="bank%d" % k) for k in range(8)]
+
+        def scores(bank, codes, scales, t, rhs, rhs_sc, h):
+            nc.tensor.matmul_mx(
+                out=bank[:],
+                lhsT=codes[:, t * P : (t + 1) * P].bitcast(FP8X4),
+                lhsT_scale=scales[:, t * P : (t + 1) * P],
+                rhs=rhs,
+                rhs_scale=rhs_sc[:, h * BANK : (h + 1) * BANK],
+                start=True,
+                stop=True,
+            )
+            return bank[:]
+
+        def fp4(words, c0, c1):
+            return words[:, 2 * c0 : 2 * c1].bitcast(FP4X4)
+
+        def empty(on_vector, dst, bank):
+            if on_vector:
+                nc.vector.tensor_copy(dst, bank)
+            else:
+                nc.scalar.copy(dst, bank)
+
+        def gather(on_vector, dst, win, lst):
+            if on_vector:
+                nc.vector.tensor_copy(dst, win[:].indirect(lst))
+            else:
+                nc.scalar.activation(dst, win[:].indirect(lst), COPY)
+
+        q_grp = sb("q_grp", [P, PACK, P, PACK], BF16)
+        q_codes = sb("q_codes", [P, Q], U32)
+        q_sc = sb("q_sc", [P, Q], U8)
+        q2_grp = sb("q2_grp", [P, PACK, P, PACK], BF16)
+        q2_codes = sb("q2_codes", [P, Q], U32)
+        q2_sc = sb("q2_sc", [P, Q], U8)
+        a = [sb("a%d" % t, [P, T], F32) for t in range(PACK)]
+        c0 = [sb("c%d" % t, [P, T], F32) for t in range(PACK)]
+        cc = [sb("cc%d" % t, [P, T], F32) for t in range(PACK)]
+        s1 = [sb("s%d" % t, [P, I], F32) for t in range(PACK)]
+        cg = [sb("cg%d" % t, [P, I], F32) for t in range(PACK)]
+        ag = [sb("ag%d" % t, [P, I], F32) for t in range(PACK)]
+        ccg = [sb("ccg%d" % t, [P, I], F32) for t in range(PACK)]
+        g = [sb("g%d" % t, [P, I], F32) for t in range(PACK)]
+        gw = sb("gw", [P, PACK, I], BF16)
+
+        def make_a(t, on_vector):
+            for h in range(2):
+                bank = scores(banks[h], q_codes, q_sc, t, keys[:, h * BANK : (h + 1) * BANK].bitcast(FP8X4), keys_sc, h)
+                empty(on_vector[h], a[t][:, h * BANK : (h + 1) * BANK], bank)
+
+        def make_c(t, on_vector):
+            for h in range(2):
+                bank = scores(banks[h + (2 if t == 0 else 0)], q2_codes, q2_sc, t, fp4(users, h * BANK, (h + 1) * BANK), users_sc, h)
+                empty(on_vector[h], c0[t][:, h * BANK : (h + 1) * BANK], bank)
+
+        def gate(t):
+            nc.scalar.activation(s1[t][:], a[t][:].indirect(l1[:]), SIGMOID, bias=thr_t[:, t : t + 1], scale=slope_t[:, t : t + 1])
+
+        def place(t):
+            win = f1[t % 2]
+            pair = [scores(banks[2 + 2 * ((t + 1) % 3) + h], q_codes, q_sc, t, fp4(notes, h * BANK, (h + 1) * BANK), notes_sc, h) for h in range(2)]
+            nc.vector.tensor_tensor(win[:].indirect(l3[:]), cg[t][:], s1[t][:], MULT)
+            for h in range(2):
+                cols = slice(h * BANK, (h + 1) * BANK)
+                nc.vector.tensor_tensor(cc[t][:, cols], pair[h], win[:, cols], ADD)
+
+        deal(q_grp, q_raw, 0)
+        deal(q_grp, q_raw, 1)
+        quantize(q_codes, q_sc, q_grp, 0, 1)
+        quantize(q_codes, q_sc, q_grp, 1, PACK)
+        make_a(0, (False, True))
+        gate(0)
+        deal(q2_grp, q2_raw, 0)
+        deal(q2_grp, q2_raw, 1)
+        quantize(q2_codes, q2_sc, q2_grp, 0, 1)
+        quantize(q2_codes, q2_sc, q2_grp, 1, PACK)
+        make_a(1, (False, False))
+        make_c(0, (True, True))
+        gather(True, cg[0][:], c0[0], l2[:])
+        place(0)
+        for t in range(1, PACK):
+            if t > 1:
+                make_a(t, (False, False))
+            gate(t)
+            make_c(t, (False, False))
+            gather(False, cg[t][:], c0[t], l2[:])
+            place(t)
+        half = I // 2
+        last = PACK - 1
+        for t in range(PACK):
+            gather(t == last, ag[t][:], a[t], l5[:])
+            pieces = 2 if t == last else 1
+            width = I // pieces
+            for k in range(pieces):
+                cols = slice(k * width, (k + 1) * width)
+                gather(False, ccg[t][:, cols], cc[t], l4[:, k * width // 16 : (k + 1) * width // 16])
+                nc.vector.tensor_tensor(g[t][:, cols], ccg[t][:, cols], ag[t][:, cols], MAX)
+            for k in range(pieces):
+                cols = slice(k * width, (k + 1) * width)
+                nc.vector.tensor_scalar(gw[:, t, cols], g[t][:, cols], rowf_t[:, t : t + 1], None, MULT)
+
+        gw_grp = [sb("gw_grp%d" % h, [P, half, PACK], BF16) for h in range(2)]
+        gw_codes = [sb("gw_codes%d" % h, [P, half], U32) for h in range(2)]
+        gw_sc = [sb("gw_sc%d" % h, [P, half], U8) for h in range(2)]
+        for h in range(2):
+            src = gw[:, :, h * half : (h + 1) * half].rearrange("p t i -> p i t")
+            if h == 0:
+                nc.vector.tensor_copy(gw_grp[h][:], src)
+            else:
+                nc.scalar.copy(gw_grp[h][:], src)
+        for h in range(2):
+            nc.vector.quantize_mx(out=gw_codes[h][:].bitcast(FP8X4), scales=gw_sc[h][:], in_=gw_grp[h][:].rearrange("p i t -> p (i t)"))
+        for h in range(2):
+            for k in range(2):
+                bank = banks[2 * h + k][:, :half]
+                nc.tensor.matmul_mx(
+                    out=bank,
+                    lhsT=fp4(mix, k * P, (k + 1) * P),
+                    lhsT_scale=mix_sc[:, k * P : (k + 1) * P],
+                    rhs=gw_codes[h][:].bitcast(FP8X4),
+                    rhs_scale=gw_sc[h][:],
+                    start=True,
+                    stop=True,
+                )
+                res = sb("res%d%d" % (h, k), [P, half], F32)
+                empty(k == 1, res[:], bank)
+                nc.sync.dma_start(out[k * P : (k + 1) * P, h * half : (h + 1) * half], res[:])

@@ -75,14 +75,18 @@ def tile_attend_upheld_threeq_mixed_kernel(
         thr_t = load_rows(nc.gpsimd, "thr_t", thr)
         rowf_t = load_rows(nc.gpsimd, "rowf_t", rowf)
         for win in f1:
-            nc.gpsimd.memset(win[:], 0.0)
+            nc.vector.memset(win[:], 0.0)
 
         load_scales(nc.scalar, keys_sc, keys_scales)
+        warm_in = sb("warm_in", [P, 8], F32)
+        warm_out = sb("warm_out", [P, 8], F32)
+        nc.vector.memset(warm_in[:], 0.0)
+        nc.scalar.activation(warm_out[:], warm_in[:], SIGMOID)
         l1 = load_list("l1", offs)
-        q_raw = load_query("q", query)
+        q_raw = load_query("q_raw", query)
         keys = sb("keys", [P, T], U32)
         nc.sync.dma_start(keys[:].bitcast(I32), keys_words[0].rearrange("p n r -> p (n r)").bitcast(I32))
-        q2_raw = load_query("q2", query2)
+        q2_raw = load_query("q2_raw", query2)
         users = load_fp4("users", users_words, T)
         load_scales(nc.sync, users_sc, users_scales)
         l2 = load_list("l2", offs2)
@@ -148,14 +152,14 @@ def tile_attend_upheld_threeq_mixed_kernel(
         cc = [sb("cc%d" % t, [P, T], F32) for t in range(PACK)]
         s1 = [sb("s%d" % t, [P, I], F32) for t in range(PACK)]
         cg = [sb("cg%d" % t, [P, I], F32) for t in range(PACK)]
-        ag = [sb("ag%d" % t, [P, I], F32) for t in range(PACK)]
+        ag = [s1[0], cg[0], s1[1], cg[1]]
         ccg = [sb("ccg%d" % t, [P, I], F32) for t in range(PACK)]
         g = [sb("g%d" % t, [P, I], F32) for t in range(PACK)]
-        gw = sb("gw", [P, PACK, I], BF16)
+        gw = sb("gw", [P, PACK - 1, I], BF16)
 
         def make_a(t, on_vector):
             for h in range(2):
-                bank = scores(banks[h], q_codes, q_sc, t, keys[:, h * BANK : (h + 1) * BANK].bitcast(FP8X4), keys_sc, h)
+                bank = scores(banks[h + (2 if t > 1 else 0)], q_codes, q_sc, t, keys[:, h * BANK : (h + 1) * BANK].bitcast(FP8X4), keys_sc, h)
                 empty(on_vector[h], a[t][:, h * BANK : (h + 1) * BANK], bank)
 
         def make_c(t, on_vector):
@@ -168,7 +172,7 @@ def tile_attend_upheld_threeq_mixed_kernel(
 
         def place(t):
             win = f1[t % 2]
-            pair = [scores(banks[2 + 2 * ((t + 1) % 3) + h], q_codes, q_sc, t, fp4(notes, h * BANK, (h + 1) * BANK), notes_sc, h) for h in range(2)]
+            pair = [scores(banks[4 + 2 * (t % 2) + h], q_codes, q_sc, t, fp4(notes, h * BANK, (h + 1) * BANK), notes_sc, h) for h in range(2)]
             nc.vector.tensor_tensor(win[:].indirect(l3[:]), cg[t][:], s1[t][:], MULT)
             for h in range(2):
                 cols = slice(h * BANK, (h + 1) * BANK)
@@ -191,33 +195,29 @@ def tile_attend_upheld_threeq_mixed_kernel(
         for t in range(1, PACK):
             if t > 1:
                 make_a(t, (False, False))
-            gate(t)
             make_c(t, (False, False))
+            gate(t)
             gather(False, cg[t][:], c0[t], l2[:])
             place(t)
         half = I // 2
         last = PACK - 1
-        for t in range(PACK):
-            gather(t == last, ag[t][:], a[t], l5[:])
-            pieces = 2 if t == last else 1
-            width = I // pieces
-            for k in range(pieces):
-                cols = slice(k * width, (k + 1) * width)
-                gather(False, ccg[t][:, cols], cc[t], l4[:, k * width // 16 : (k + 1) * width // 16])
-                nc.vector.tensor_tensor(g[t][:, cols], ccg[t][:, cols], ag[t][:, cols], MAX)
-            for k in range(pieces):
-                cols = slice(k * width, (k + 1) * width)
-                nc.vector.tensor_scalar(gw[:, t, cols], g[t][:, cols], rowf_t[:, t : t + 1], None, MULT)
-
         gw_grp = [sb("gw_grp%d" % h, [P, half, PACK], BF16) for h in range(2)]
         gw_codes = [sb("gw_codes%d" % h, [P, half], U32) for h in range(2)]
         gw_sc = [sb("gw_sc%d" % h, [P, half], U8) for h in range(2)]
+        for t in range(last):
+            gather(False, ag[t][:], a[t], l5[:])
+            gather(False, ccg[t][:], cc[t], l4[:])
+            nc.vector.tensor_tensor(g[t][:], ccg[t][:], ag[t][:], MAX)
+            nc.vector.tensor_scalar(gw[:, t, :], g[t][:], rowf_t[:, t : t + 1], None, MULT)
         for h in range(2):
-            src = gw[:, :, h * half : (h + 1) * half].rearrange("p t i -> p i t")
-            if h == 0:
-                nc.vector.tensor_copy(gw_grp[h][:], src)
-            else:
-                nc.scalar.copy(gw_grp[h][:], src)
+            nc.vector.tensor_copy(gw_grp[h][:, :, :last], gw[:, :, h * half : (h + 1) * half].rearrange("p t i -> p i t"))
+        gather(False, ag[last][:], a[last], l5[:])
+        for h in range(2):
+            cols = slice(h * half, (h + 1) * half)
+            gather(False, ccg[last][:, cols], cc[last], l4[:, h * half // 16 : (h + 1) * half // 16])
+            nc.vector.tensor_tensor(g[last][:, cols], ccg[last][:, cols], ag[last][:, cols], MAX)
+        for h in range(2):
+            nc.vector.tensor_scalar(gw_grp[h][:, :, last], g[last][:, h * half : (h + 1) * half], rowf_t[:, last : last + 1], None, MULT)
         for h in range(2):
             nc.vector.quantize_mx(out=gw_codes[h][:].bitcast(FP8X4), scales=gw_sc[h][:], in_=gw_grp[h][:].rearrange("p i t -> p (i t)"))
         for h in range(2):

@@ -159,12 +159,12 @@ def tile_attend_upheld_threeq_mixed_kernel(
 
         def make_a(t, on_vector):
             for h in range(2):
-                bank = scores(banks[h + (2 if t > 1 else 0)], q_codes, q_sc, t, keys[:, h * BANK : (h + 1) * BANK].bitcast(FP8X4), keys_sc, h)
+                bank = scores(banks[2 * (0, 0, 2, 1)[t] + h], q_codes, q_sc, t, keys[:, h * BANK : (h + 1) * BANK].bitcast(FP8X4), keys_sc, h)
                 empty(on_vector[h], a[t][:, h * BANK : (h + 1) * BANK], bank)
 
         def make_c(t, on_vector):
             for h in range(2):
-                bank = scores(banks[h + (2 if t == 0 else 0)], q2_codes, q2_sc, t, fp4(users, h * BANK, (h + 1) * BANK), users_sc, h)
+                bank = scores(banks[2 * (1, 0, 2, 2)[t] + h], q2_codes, q2_sc, t, fp4(users, h * BANK, (h + 1) * BANK), users_sc, h)
                 empty(on_vector[h], c0[t][:, h * BANK : (h + 1) * BANK], bank)
 
         def gate(t):
@@ -172,7 +172,7 @@ def tile_attend_upheld_threeq_mixed_kernel(
 
         def place(t):
             win = f1[t % 2]
-            pair = [scores(banks[4 + 2 * (t % 2) + h], q_codes, q_sc, t, fp4(notes, h * BANK, (h + 1) * BANK), notes_sc, h) for h in range(2)]
+            pair = [scores(banks[2 * (t % 2) + h], q_codes, q_sc, t, fp4(notes, h * BANK, (h + 1) * BANK), notes_sc, h) for h in range(2)]
             nc.vector.tensor_tensor(win[:].indirect(l3[:]), cg[t][:], s1[t][:], MULT)
             for h in range(2):
                 cols = slice(h * BANK, (h + 1) * BANK)
@@ -191,14 +191,14 @@ def tile_attend_upheld_threeq_mixed_kernel(
         make_a(1, (False, False))
         make_c(0, (True, True))
         gather(True, cg[0][:], c0[0], l2[:])
-        place(0)
         for t in range(1, PACK):
-            if t > 1:
-                make_a(t, (False, False))
-            make_c(t, (False, False))
             gate(t)
+            if t + 1 < PACK:
+                make_a(t + 1, (False, False))
+            make_c(t, (False, False))
             gather(False, cg[t][:], c0[t], l2[:])
-            place(t)
+            place(t - 1)
+        place(PACK - 1)
         half = I // 2
         last = PACK - 1
         gw_grp = [sb("gw_grp%d" % h, [P, half, PACK], BF16) for h in range(2)]
@@ -222,7 +222,7 @@ def tile_attend_upheld_threeq_mixed_kernel(
             nc.vector.quantize_mx(out=gw_codes[h][:].bitcast(FP8X4), scales=gw_sc[h][:], in_=gw_grp[h][:].rearrange("p i t -> p (i t)"))
         for h in range(2):
             for k in range(2):
-                bank = banks[2 * h + k][:, :half]
+                bank = banks[4 + 2 * h + k][:, :half]
                 nc.tensor.matmul_mx(
                     out=bank,
                     lhsT=fp4(mix, k * P, (k + 1) * P),

from contextlib import ExitStack

import concourse.mybir as mybir

D, T, Q, I, E = 512, 1024, 512, 512, 256
P = 128
PACK = 4
BANK = 512
FLOPS = 2 * D * Q * T * 3 + 2 * Q * E * I

F32 = mybir.dt.float32
BF16 = mybir.dt.bfloat16
I32 = mybir.dt.int32
U32 = mybir.dt.uint32
U16 = mybir.dt.uint16
U8 = mybir.dt.uint8
FP8X4 = mybir.dt.float8_e4m3fn_x4
FP4X4 = mybir.dt.float4_e2m1fn_x4
MULT = mybir.AluOpType.mult
ADD = mybir.AluOpType.add
MAX = mybir.AluOpType.max
COPY = mybir.ActivationFunctionType.Copy
SIGMOID = mybir.ActivationFunctionType.Sigmoid


def tile_attend_upheld_threeq_mixed_kernel(
    tc, query, query2, keys_words, keys_scales, notes_words, notes_scales, users_words, users_scales,
    thr, slope, rowf, mix_words, mix_scales, offs, offs2, offs3, offs4, offs5, out,
):
    nc = tc.nc
    with ExitStack() as ctx:
        keep = ctx.enter_context(tc.tile_pool(name="keep", bufs=1))
        psum = ctx.enter_context(tc.psum_pool(name="psum", bufs=1))

        def sb(name, shape, dtype):
            return keep.tile(shape, dtype, name=name, align_bytes=64)

        def scale_plane(name, width):
            plane = sb(name, [P, width], U8)
            return plane

        def load_scales(queue, plane, scales):
            for quad in range(4):
                queue.dma_start(plane[32 * quad : 32 * quad + 4, :].bitcast(I32), scales[0, 4 * quad : 4 * quad + 4, :].bitcast(I32))

        def load_list(name, src):
            lst = sb(name, [P, I // 16], U16)
            nc.sync.dma_start(lst[:], src)
            return lst

        def load_rows(queue, name, src):
            col = sb(name, [P, PACK], F32)
            queue.dma_start(col[:], src.rearrange("(p t) o -> p (t o)", t=PACK))
            return col

        def load_query(name, src):
            halves = []
            for h in range(2):
                raw = sb("%s_raw%d" % (name, h), [P, PACK, Q // 2], F32)
                nc.sync.dma_start(raw[:], src.rearrange("(p j) q -> p j q", j=PACK)[:, :, h * (Q // 2) : (h + 1) * (Q // 2)])
                halves.append(raw)
            return halves

        def load_fp4(name, src, width):
            words = sb(name, [P, 2 * width], U8)
            nc.sync.dma_start(words[:].bitcast(I32), src[0].bitcast(I32))
            return words

        keys_sc = scale_plane("keys_sc", T)
        users_sc = scale_plane("users_sc", T)
        notes_sc = scale_plane("notes_sc", T)
        mix_sc = scale_plane("mix_sc", E)
        f1 = [sb("f1_%d" % k, [P, T], F32) for k in range(2)]
        slope_t = load_rows(nc.gpsimd, "slope_t", slope)
        thr_t = load_rows(nc.gpsimd, "thr_t", thr)
        rowf_t = load_rows(nc.gpsimd, "rowf_t", rowf)
        for win in f1:
            nc.vector.memset(win[:], 0.0)

        load_scales(nc.scalar, keys_sc, keys_scales)
        warm_in = sb("warm_in", [P, 8], F32)
        warm_out = sb("warm_out", [P, 8], F32)
        nc.vector.memset(warm_in[:], 0.0)
        nc.scalar.activation(warm_out[:], warm_in[:], SIGMOID)
        l1 = load_list("l1", offs)
        q_raw = load_query("q_raw", query)
        keys = sb("keys", [P, T], U32)
        nc.sync.dma_start(keys[:].bitcast(I32), keys_words[0].rearrange("p n r -> p (n r)").bitcast(I32))
        q2_raw = load_query("q2_raw", query2)
        users = load_fp4("users", users_words, T)
        load_scales(nc.sync, users_sc, users_scales)
        l2 = load_list("l2", offs2)
        l3 = load_list("l3", offs3)
        notes = load_fp4("notes", notes_words, T)
        load_scales(nc.sync, notes_sc, notes_scales)
        l5 = load_list("l5", offs5)
        l4 = load_list("l4", offs4)
        mix = load_fp4("mix", mix_words, E)
        load_scales(nc.sync, mix_sc, mix_scales)

        def deal(grouped, raw, h):
            m = P // 2
            nc.vector.tensor_copy(
                grouped[:, :, h * m : (h + 1) * m, :].rearrange("p t m j -> p m t j"),
                raw[h][:].rearrange("p j (m t) -> p m t j", t=PACK),
            )

        def quantize(codes, scales, grouped, t0, t1):
            nc.vector.quantize_mx(
                out=codes[:, t0 * P : t1 * P].bitcast(FP8X4),
                scales=scales[:, t0 * P : t1 * P],
                in_=grouped[:, t0:t1, :, :].rearrange("p t m j -> p (t m j)"),
            )

        banks = [psum.tile([P, BANK], F32, name="bank%d" % k) for k in range(8)]

        def scores(bank, codes, scales, t, rhs, rhs_sc, h):
            nc.tensor.matmul_mx(
                out=bank[:],
                lhsT=codes[:, t * P : (t + 1) * P].bitcast(FP8X4),
                lhsT_scale=scales[:, t * P : (t + 1) * P],
                rhs=rhs,
                rhs_scale=rhs_sc[:, h * BANK : (h + 1) * BANK],
                start=True,
                stop=True,
            )
            return bank[:]

        def fp4(words, c0, c1):
            return words[:, 2 * c0 : 2 * c1].bitcast(FP4X4)

        def empty(on_vector, dst, bank):
            if on_vector:
                nc.vector.tensor_copy(dst, bank)
            else:
                nc.scalar.copy(dst, bank)

        def gather(on_vector, dst, win, lst):
            if on_vector:
                nc.vector.tensor_copy(dst, win[:].indirect(lst))
            else:
                nc.scalar.activation(dst, win[:].indirect(lst), COPY)

        q_grp = sb("q_grp", [P, PACK, P, PACK], BF16)
        q_codes = sb("q_codes", [P, Q], U32)
        q_sc = sb("q_sc", [P, Q], U8)
        q2_grp = sb("q2_grp", [P, PACK, P, PACK], BF16)
        q2_codes = sb("q2_codes", [P, Q], U32)
        q2_sc = sb("q2_sc", [P, Q], U8)
        a = [sb("a%d" % t, [P, T], F32) for t in range(PACK)]
        c0 = [sb("c%d" % t, [P, T], F32) for t in range(PACK)]
        cc = [sb("cc%d" % t, [P, T], F32) for t in range(PACK)]
        s1 = [sb("s%d" % t, [P, I], F32) for t in range(PACK)]
        cg = [sb("cg%d" % t, [P, I], F32) for t in range(PACK)]
        ag = [s1[0], cg[0], s1[1], cg[1]]
        ccg = [sb("ccg%d" % t, [P, I], F32) for t in range(PACK)]
        g = [sb("g%d" % t, [P, I], F32) for t in range(PACK)]
        gw = sb("gw", [P, PACK - 1, I], BF16)

        def make_a(t, on_vector):
            for h in range(2):
                bank = scores(banks[2 * (0, 0, 2, 1)[t] + h], q_codes, q_sc, t, keys[:, h * BANK : (h + 1) * BANK].bitcast(FP8X4), keys_sc, h)
                empty(on_vector[h], a[t][:, h * BANK : (h + 1) * BANK], bank)

        def make_c(t, on_vector):
            for h in range(2):
                bank = scores(banks[2 * (1, 0, 2, 2)[t] + h], q2_codes, q2_sc, t, fp4(users, h * BANK, (h + 1) * BANK), users_sc, h)
                empty(on_vector[h], c0[t][:, h * BANK : (h + 1) * BANK], bank)

        def gate(t):
            nc.scalar.activation(s1[t][:], a[t][:].indirect(l1[:]), SIGMOID, bias=thr_t[:, t : t + 1], scale=slope_t[:, t : t + 1])

        def place(t):
            win = f1[t % 2]
            pair = [scores(banks[2 * (t % 2) + h], q_codes, q_sc, t, fp4(notes, h * BANK, (h + 1) * BANK), notes_sc, h) for h in range(2)]
            nc.vector.tensor_tensor(win[:].indirect(l3[:]), cg[t][:], s1[t][:], MULT)
            for h in range(2):
                cols = slice(h * BANK, (h + 1) * BANK)
                nc.vector.tensor_tensor(cc[t][:, cols], pair[h], win[:, cols], ADD)

        deal(q_grp, q_raw, 0)
        deal(q_grp, q_raw, 1)
        quantize(q_codes, q_sc, q_grp, 0, 1)
        quantize(q_codes, q_sc, q_grp, 1, PACK)
        make_a(0, (False, True))
        gate(0)
        deal(q2_grp, q2_raw, 0)
        deal(q2_grp, q2_raw, 1)
        quantize(q2_codes, q2_sc, q2_grp, 0, 1)
        quantize(q2_codes, q2_sc, q2_grp, 1, PACK)
        make_a(1, (False, False))
        make_c(0, (True, True))
        gather(True, cg[0][:], c0[0], l2[:])
        for t in range(1, PACK):
            gate(t)
            if t + 1 < PACK:
                make_a(t + 1, (False, False))
            make_c(t, (False, False))
            gather(False, cg[t][:], c0[t], l2[:])
            place(t - 1)
        place(PACK - 1)
        half = I // 2
        last = PACK - 1
        gw_grp = [sb("gw_grp%d" % h, [P, half, PACK], BF16) for h in range(2)]
        gw_codes = [sb("gw_codes%d" % h, [P, half], U32) for h in range(2)]
        gw_sc = [sb("gw_sc%d" % h, [P, half], U8) for h in range(2)]
        for t in range(last):
            gather(False, ag[t][:], a[t], l5[:])
            gather(False, ccg[t][:], cc[t], l4[:])
            nc.vector.tensor_tensor(g[t][:], ccg[t][:], ag[t][:], MAX)
            nc.vector.tensor_scalar(gw[:, t, :], g[t][:], rowf_t[:, t : t + 1], None, MULT)
        for h in range(2):
            nc.vector.tensor_copy(gw_grp[h][:, :, :last], gw[:, :, h * half : (h + 1) * half].rearrange("p t i -> p i t"))
        gather(False, ag[last][:], a[last], l5[:])
        for h in range(2):
            cols = slice(h * half, (h + 1) * half)
            gather(False, ccg[last][:, cols], cc[last], l4[:, h * half // 16 : (h + 1) * half // 16])
            nc.vector.tensor_tensor(g[last][:, cols], ccg[last][:, cols], ag[last][:, cols], MAX)
        for h in range(2):
            nc.vector.tensor_scalar(gw_grp[h][:, :, last], g[last][:, h * half : (h + 1) * half], rowf_t[:, last : last + 1], None, MULT)
        for h in range(2):
            nc.vector.quantize_mx(out=gw_codes[h][:].bitcast(FP8X4), scales=gw_sc[h][:], in_=gw_grp[h][:].rearrange("p i t -> p (i t)"))
        for h in range(2):
            for k in range(2):
                bank = banks[4 + 2 * h + k][:, :half]
                nc.tensor.matmul_mx(
                    out=bank,
                    lhsT=fp4(mix, k * P, (k + 1) * P),
                    lhsT_scale=mix_sc[:, k * P : (k + 1) * P],
                    rhs=gw_codes[h][:].bitcast(FP8X4),
                    rhs_scale=gw_sc[h][:],
                    start=True,
                    stop=True,
                )
                res = sb("res%d%d" % (h, k), [P, half], F32)
                empty(k == 1, res[:], bank)
                nc.sync.dma_start(out[k * P : (k + 1) * P, h * half : (h + 1) * half], res[:])
